import numpy as np
import ml_dtypes


def mxq(x, axis, fmt="e4m3"):
    dtype, down = {"e4m3": (ml_dtypes.float8_e4m3fn, 7), "e5m2": (ml_dtypes.float8_e5m2, 14)}[fmt]
    v = np.moveaxis(np.asarray(x, np.float32).astype(ml_dtypes.bfloat16).astype(np.float64), axis, -1)
    blocks = v.reshape(v.shape[:-1] + (-1, 32))
    amax = np.abs(blocks).max(-1, keepdims=True)
    byte = np.maximum(np.where(amax > 0, np.frexp(amax)[1] - 1 + 127, 0) - down, 1)
    scale = np.exp2(byte - 127.0)
    codes = (blocks / scale).astype(np.float32).astype(dtype).astype(np.float64)
    return np.moveaxis((codes * scale).reshape(v.shape), -1, axis)


WIDE = False


def mx_kscale(k):
    if not WIDE:
        return np.ones(k)
    levels = np.array([10, -10, 5, -5, 0])
    if k % 512:
        return np.exp2(np.random.permutation(np.resize(levels, k // 32))).repeat(32)
    a = np.empty((k // 512, 16))
    for p in range(k // 512):
        a[p, :8] = np.random.permutation(np.resize(levels, 8))
        for g in range(8):
            far = levels[np.abs(levels - a[p, g]) >= 10]
            a[p, g + 8] = far[np.random.randint(len(far))]
    return np.exp2(a.ravel()).repeat(32)


def f64(x):
    return np.asarray(x).astype(np.float64)


def striped(idx):
    return np.tile(idx.reshape(-1, 16).T, (8, 1)).astype(np.uint16)


def unstriped(offs):
    return offs[:16].T.reshape(-1).astype(np.int64)


E2M1 = np.array([0.0, 0.5, 1.0, 1.5, 2.0, 3.0, 4.0, 6.0, -0.0, -0.5, -1.0, -1.5, -2.0, -3.0, -4.0, -6.0])


def pack_weight(w, fmt):
    k, n = w.shape
    w = f64(np.asarray(w, np.float32).astype(ml_dtypes.bfloat16)).reshape(k // 32, 32, n)
    amax = np.abs(w).max(1)
    if fmt == "e4m3":
        byte = np.frexp(amax)[1] - 1 + 127 - 7
    else:
        mant, ex = np.frexp(amax / 6.0)
        byte = np.where(mant > 0.5, ex, ex - 1) + 127
    byte = np.clip(np.where(amax > 0, byte, 1), 1, 254)
    scaled = (w * np.exp2(127.0 - byte)[:, None, :]).reshape(k, n).astype(np.float32)
    by_word = np.ascontiguousarray(scaled.reshape(k // 512, 128, 4, n).transpose(0, 1, 3, 2))
    if fmt == "e4m3":
        words = by_word.astype(ml_dtypes.float8_e4m3fn).view(np.uint8)
    else:
        c = by_word.astype(ml_dtypes.float4_e2m1fn).view(np.uint8) & 0xF
        words = (c[..., 0::2] | (c[..., 1::2] << 4)).reshape(k // 512, 128, 2 * n)
    return np.ascontiguousarray(words), np.ascontiguousarray(byte.astype(np.uint8).reshape(k // 512, 16, n))


def unpack_weight(words, scales, fmt):
    g, _, n = scales.shape
    words = np.ascontiguousarray(words).reshape(g, 128, n, -1)
    if fmt == "e4m3":
        vals = words.view(ml_dtypes.float8_e4m3fn).astype(np.float64)
    else:
        nib = np.empty((g, 128, n, 4), np.uint8)
        nib[..., 0::2] = words & 0xF
        nib[..., 1::2] = words >> 4
        vals = E2M1[nib]
    vals = vals * np.repeat(np.exp2(scales.astype(np.float64) - 127.0), 8, axis=1)[..., None]
    return vals.transpose(0, 1, 3, 2).reshape(g * 512, n)


def gelu(v):
    return 0.5 * v * (1.0 + np.tanh(np.sqrt(2.0 / np.pi) * (v + 0.044715 * v**3)))


K, T, S, H, T2, P = 1536, 2048, 1024, 512, 2048, 512


def setup_inputs():
    n = np.random.standard_normal
    s = mx_kscale(K)[:, None]
    u = mx_kscale(H)[:, None]
    tab_words, tab_scales = pack_weight(n((K, T)) * s, "e4m3")
    w4_words, w4_scales = pack_weight(n((K, H)) / np.sqrt(K) / s * u.T, "e2m1")
    return {
        "tab_words": tab_words, "tab_scales": tab_scales,
        "offs": striped(np.random.permutation(T)[:S]),
        "w1": (n((K, H)) / np.sqrt(K) / s * u.T).astype(np.float32),
        "w4_words": w4_words, "w4_scales": w4_scales,
        "page0": (n((H, T2)) * u).astype(np.float32),
        "offs2": striped(np.random.permutation(T2)[:S]),
        "wgs": np.exp(0.3 * n((128, S))).astype(np.float32),
        "offs3": striped(np.random.permutation(T2)[:P]),
        "offs4": striped(np.random.permutation(T2)[:P]),
        "base": (0.6 * n(H) * u[:, 0]).astype(np.float32),
        "gain": (1.2 * n(H) / np.sqrt(H) / u[:, 0] ** 2).astype(np.float32),
        "pair": n((P, P)).astype(np.float32),
    }


def reference(tab_words, tab_scales, offs, w1, w4_words, w4_scales, page0, offs2, wgs, offs3, offs4, base, gain, pair):
    v = unpack_weight(tab_words, tab_scales, "e4m3")[:, unstriped(offs)]
    w4 = unpack_weight(w4_words, w4_scales, "e2m1")
    h1 = mxq(f64(w1), 0, "e4m3").T @ v
    h2 = w4.T @ v
    h = np.maximum(h1, h2)
    page = f64(page0).copy()
    page[:, unstriped(offs2)] = np.tile(f64(wgs), (H // 128, 1)) * h
    x1 = page[:, unstriped(offs3)]
    x2 = (page[:, unstriped(offs4)] - f64(base)[:, None]) * f64(gain)[:, None]
    e = mxq(x1, 0, "e4m3").T @ mxq(x2, 0, "e4m3")
    return np.tanh(e) * f64(pair)

@@ -1,0 +1,250 @@
+from contextlib import ExitStack
+
+import concourse.mybir as mybir
+
+K, T, S, H, T2, NP = 1536, 2048, 1024, 512, 2048, 512
+FLOPS = 2 * (2 * K * H * S + H * NP * NP)
+
+F32 = mybir.dt.float32
+BF16 = mybir.dt.bfloat16
+I32 = mybir.dt.int32
+U32 = mybir.dt.uint32
+U16 = mybir.dt.uint16
+U8 = mybir.dt.uint8
+FP8X4 = mybir.dt.float8_e4m3fn_x4
+FP4X4 = mybir.dt.float4_e2m1fn_x4
+ALU = mybir.AluOpType
+ACT = mybir.ActivationFunctionType
+
+P = 128
+PACK = 4
+PASSES = K // (P * PACK)
+BANK = 512
+QUADS = 4
+
+
+def tile_list_coating_adhesion_chart_kernel(
+    tc, tab_words, tab_scales, offs, w1, w4_words, w4_scales, page0, offs2, wgs, offs3, offs4, base, gain, pair, out
+):
+    nc = tc.nc
+    with ExitStack() as ctx:
+        keep = ctx.enter_context(tc.tile_pool(name="keep", bufs=1))
+        ring = ctx.enter_context(tc.tile_pool(name="ring", bufs=2))
+        psum = ctx.enter_context(tc.psum_pool(name="psum", bufs=2))
+
+        pick = keep.tile([P, S // 16], U16, name="pick")
+        nc.sync.dma_start(pick[:], offs)
+
+        def load_table(a):
+            tw = keep.tile([P, T], I32, name=f"tab_w{a}", align_bytes=64)
+            nc.sync.dma_start(tw[:], tab_words[a].rearrange("p t i -> p (t i)").bitcast(I32))
+            return tw
+
+        tab_w = [load_table(0)]
+        tab_s = keep.tile([P, T], U8, name="tab_s", align_bytes=64)
+        nc.gpsimd.memset(tab_s[:].bitcast(I32), 0)
+        w4_s_raw = keep.tile([P, PASSES, H], U8, name="w4_s_raw", align_bytes=64)
+        nc.vector.memset(w4_s_raw[:].bitcast(I32), 0)
+        for q in range(QUADS):
+            nc.sync.dma_start(
+                tab_s[32 * q : 32 * q + 4 * PASSES, :].bitcast(I32), tab_scales[:, 4 * q : 4 * q + 4, :].bitcast(I32)
+            )
+        tab_w.extend(load_table(a) for a in range(1, PASSES))
+        for q in range(QUADS):
+            nc.sync.dma_start(
+                w4_s_raw[32 * q : 32 * q + 4, :, :].bitcast(I32),
+                w4_scales[:, 4 * q : 4 * q + 4, :].rearrange("a r c -> r a c").bitcast(I32),
+            )
+        w4_w_raw = keep.tile([P, PASSES, H // 2], I32, name="w4_w_raw", align_bytes=64)
+        nc.sync.dma_start(w4_w_raw[:], w4_words.bitcast(I32).rearrange("a p w -> p a w"))
+        w1_raw = []
+        for a in range(PASSES):
+            wr = keep.tile([P, PACK, H], F32, name=f"w1_raw{a}")
+            nc.sync.dma_start(wr[:], w1[512 * a : 512 * (a + 1), :].rearrange("(p j) c -> p j c", j=PACK))
+            w1_raw.append(wr)
+
+        page_rows = page0.rearrange("(q t e) c -> t q e c", t=PACK, e=2)
+        wgs_rows = wgs.rearrange("(q t e) j -> t q e j", t=PACK, e=2)
+        put = keep.tile([P, S // 16], U16, name="put")
+        take1 = keep.tile([P, NP // 16], U16, name="take1")
+        take2 = keep.tile([P, NP // 16], U16, name="take2")
+        base_sb = keep.tile([P, PACK], F32, name="base_sb")
+        gain_sb = keep.tile([P, PACK], F32, name="gain_sb")
+        pages, weights = [], []
+        for t in range(PACK):
+            wg = keep.tile([P, S], F32, name=f"wgs{t}")
+            for q in range(QUADS):
+                nc.sync.dma_start(wg[32 * q : 32 * (q + 1), :], wgs_rows[t])
+            weights.append(wg)
+            if t == 0:
+                nc.sync.dma_start(put[:], offs2)
+            pg = keep.tile([P, T2], F32, name=f"page{t}")
+            nc.sync.dma_start(pg[:], page_rows[t])
+            pages.append(pg)
+            if t == 0:
+                nc.sync.dma_start(take1[:], offs3)
+                nc.sync.dma_start(take2[:], offs4)
+            if t == 1:
+                with nc.allow_non_contiguous_dma(reason="one value for each row of the page"):
+                    for e in range(2):
+                        nc.sync.dma_start(base_sb[e:P:2, :], base.rearrange("(q t e) -> e q t", t=PACK, e=2)[e])
+                        nc.sync.dma_start(gain_sb[e:P:2, :], gain.rearrange("(q t e) -> e q t", t=PACK, e=2)[e])
+        pair_sb = keep.tile([P, NP // P, NP], F32, name="pair_sb")
+        nc.sync.dma_start(pair_sb[:], pair.rearrange("(c p) j -> p c j", p=P))
+
+        v_s_low = []
+        for a in range(1, PASSES):
+            sh = keep.tile([P, S], U8, name=f"v_s_low{a}", align_bytes=64)
+            nc.vector.memset(sh[:].bitcast(I32), 0)
+            v_s_low.append(sh)
+
+        def gather_words(a, tag):
+            vw = keep.tile([P, S], U32, name=f"v_w{a}", tag=tag, align_bytes=64)
+            nc.vector.tensor_copy(vw[:], tab_w[a][:].bitcast(U32).indirect(pick[:]))
+            return vw
+
+        v_w = [gather_words(0, "v_w0")]
+        v_s = keep.tile([P, S], U8, name="v_s", tag="tab_w0", align_bytes=64)
+        nc.vector.tensor_copy(v_s[:], tab_s[:].indirect(pick[:]))
+        v_s0 = [v_s] + v_s_low
+        for a in range(1, PASSES):
+            nc.gpsimd.dma_start(v_s0[a][0:112, :].bitcast(I32), v_s[4 * a : 4 * a + 112, :].bitcast(I32))
+        v_w.append(gather_words(1, "tab_s"))
+
+        w4_w = keep.tile([P, PASSES * 2 * H], U8, name="w4_w", tag="tab_w1", align_bytes=64)
+        nc.vector.tensor_copy(
+            w4_w[:].bitcast(I32).rearrange("p (a t q) -> p a q t", a=PASSES, t=PACK),
+            w4_w_raw[:].rearrange("p a (q t) -> p a q t", t=PACK),
+        )
+        w4_s = keep.tile([P, PASSES * H], U8, name="w4_s", tag="w4_w_raw", align_bytes=64)
+        nc.vector.tensor_copy(
+            w4_s[:].bitcast(U16).rearrange("p (a t q) -> p a q t", a=PASSES, t=PACK),
+            w4_s_raw[:].bitcast(U16).rearrange("p a (q t) -> p a q t", t=PACK),
+        )
+
+        v_w.append(gather_words(2, "w4_s_raw"))
+
+        w1_bf = {}
+
+        def round_w1(a, t):
+            tag = f"stage{a - 1}" if t == 0 and a > 0 else f"w1_bf{a}_{t}"
+            rounded = keep.tile([P, P * PACK], BF16, name=f"w1_bf{a}_{t}", tag=tag, align_bytes=64)
+            nc.scalar.copy(
+                rounded[:].rearrange("p (q e j) -> p q j e", e=2, j=PACK),
+                w1_raw[a][:].rearrange("p j (q t e) -> p t q j e", t=PACK, e=2)[:, t],
+            )
+            w1_bf[a, t] = rounded
+
+        def quantise_w1(t):
+            codes = keep.tile([P, PASSES * P], U32, name=f"w1_c{t}", tag="tab_w2", align_bytes=64)
+            planes = keep.tile([P, PASSES * P], U8, name=f"w1_s{t}", tag="w1_s", align_bytes=64)
+            for a in range(PASSES):
+                cols = slice(a * P, (a + 1) * P)
+                nc.vector.quantize_mx(out=codes[:, cols].bitcast(FP8X4), scales=planes[:, cols], in_=w1_bf[a, t][:])
+            return codes, planes
+
+        def first_stage(t, codes, planes):
+            h2_sb = []
+            for half in range(S // BANK):
+                cols = slice(half * BANK, (half + 1) * BANK)
+                h2 = psum.tile([P, BANK], F32, name="h2", tag=f"acc{min(t, 1)}")
+                for a in range(PASSES):
+                    g = a * PACK + t
+                    nc.tensor.matmul_mx(
+                        out=h2[:],
+                        lhsT=w4_w[:, 2 * P * g : 2 * P * (g + 1)].bitcast(FP4X4),
+                        lhsT_scale=w4_s[:, P * g : P * (g + 1)],
+                        rhs=v_w[a][:, cols].bitcast(FP8X4),
+                        rhs_scale=v_s0[a][:, cols],
+                        start=(a == 0),
+                        stop=(a == PASSES - 1),
+                    )
+                hs = keep.tile([P, BANK], F32, name="h2_sb", tag=f"stage{half}", align_bytes=64)
+                nc.scalar.copy(hs[:], h2[:])
+                h2_sb.append(hs)
+            h = keep.tile([P, S], F32, name="h")
+            for half in range(S // BANK):
+                cols = slice(half * BANK, (half + 1) * BANK)
+                h1 = psum.tile([P, BANK], F32, name="h1", tag=f"acc{1 - min(t, 1)}")
+                for a in range(PASSES):
+                    nc.tensor.matmul_mx(
+                        out=h1[:],
+                        lhsT=codes[:, a * P : (a + 1) * P].bitcast(FP8X4),
+                        lhsT_scale=planes[:, a * P : (a + 1) * P],
+                        rhs=v_w[a][:, cols].bitcast(FP8X4),
+                        rhs_scale=v_s[4 * a : P, cols],
+                        start=(a == 0),
+                        stop=(a == PASSES - 1),
+                    )
+                nc.vector.tensor_tensor(h[:, cols], h1[:], h2_sb[half][:], ALU.max)
+            return h
+
+        def put_rows(t, h):
+            nc.vector.tensor_tensor(pages[t][:].indirect(put[:]), h[:], weights[t][:], ALU.mult)
+
+        x1 = keep.tile([P, NP, PACK], BF16, name="x1", align_bytes=64)
+        x2 = keep.tile([P, NP, PACK], BF16, name="x2", align_bytes=64)
+
+        def take_rows(t):
+            pieces = 2 if t == PACK - 1 else 1
+            width = NP // pieces
+            g2 = keep.tile([P, NP], F32, name="g2", tag="stage0", align_bytes=64)
+            g1 = keep.tile([P, NP], F32, name="g1", tag="stage1", align_bytes=64)
+            above = ring.tile([P, NP], F32, name="above")
+            for i in range(pieces):
+                cols = slice(i * width, (i + 1) * width)
+                entries = slice(i * width // 16, (i + 1) * width // 16)
+                nc.vector.tensor_copy(g2[:, cols], pages[t][:].indirect(take2[:, entries]))
+                nc.scalar.activation(above[:, cols], g2[:, cols], ACT.Identity, bias=base_sb[:, t : t + 1], scale=-1.0)
+                nc.scalar.activation(x2[:, cols, t], above[:, cols], ACT.Copy, scale=gain_sb[:, t : t + 1])
+            for i in range(pieces):
+                cols = slice(i * width, (i + 1) * width)
+                entries = slice(i * width // 16, (i + 1) * width // 16)
+                nc.vector.tensor_copy(g1[:, cols], pages[t][:].indirect(take1[:, entries]))
+                nc.scalar.copy(x1[:, cols, t], g1[:, cols])
+
+        for a in range(PASSES - 1):
+            round_w1(a, 0)
+            round_w1(a, 1)
+        round_w1(PASSES - 1, 0)
+        h_now = first_stage(0, *quantise_w1(0))
+        round_w1(PASSES - 1, 1)
+        w1_next = quantise_w1(1)
+        put_rows(0, h_now)
+        for t in range(PACK):
+            h_next = first_stage(t + 1, *w1_next) if t + 1 < PACK else None
+            if t + 2 < PACK:
+                for a in range(PASSES):
+                    round_w1(a, t + 2)
+                w1_next = quantise_w1(t + 2)
+            take_rows(t)
+            if h_next is not None:
+                put_rows(t + 1, h_next)
+
+        x2_c = keep.tile([P, NP], U32, name="x2_c", align_bytes=64)
+        x2_s = keep.tile([P, NP], U8, name="x2_s", align_bytes=64)
+        nc.vector.quantize_mx(out=x2_c[:].bitcast(FP8X4), scales=x2_s[:], in_=x2[:].rearrange("p m t -> p (m t)"))
+        x1_c = keep.tile([P, NP], U32, name="x1_c", align_bytes=64)
+        x1_s = keep.tile([P, NP], U8, name="x1_s", align_bytes=64)
+        for c in range(NP // P):
+            rows = slice(c * P, (c + 1) * P)
+            nc.vector.quantize_mx(
+                out=x1_c[:, rows].bitcast(FP8X4), scales=x1_s[:, rows], in_=x1[:, rows, :].rearrange("p m t -> p (m t)")
+            )
+        for c in range(NP // P):
+            rows = slice(c * P, (c + 1) * P)
+            e = psum.tile([P, NP], F32, name="e", bufs=4)
+            nc.tensor.matmul_mx(
+                out=e[:],
+                lhsT=x1_c[:, rows].bitcast(FP8X4),
+                lhsT_scale=x1_s[:, rows],
+                rhs=x2_c[:].bitcast(FP8X4),
+                rhs_scale=x2_s[:],
+                start=True,
+                stop=True,
+            )
+            bounded = ring.tile([P, NP], F32, name="bounded", bufs=4)
+            nc.scalar.activation(bounded[:], e[:], ACT.Tanh, scale=-1.0)
+            chart = ring.tile([P, NP], F32, name="chart", bufs=4)
+            nc.vector.tensor_tensor(chart[:], bounded[:], pair_sb[:, c, :], ALU.mult)
+            nc.sync.dma_start(out[rows, :], chart[:])

@@ -44,7 +44,7 @@ def tile_list_coating_adhesion_chart_kernel(
         tab_s = keep.tile([P, T], U8, name="tab_s", align_bytes=64)
         nc.gpsimd.memset(tab_s[:].bitcast(I32), 0)
         w4_s_raw = keep.tile([P, PASSES, H], U8, name="w4_s_raw", align_bytes=64)
-        nc.vector.memset(w4_s_raw[:].bitcast(I32), 0)
+        nc.gpsimd.memset(w4_s_raw[:].bitcast(I32), 0)
         for q in range(QUADS):
             nc.sync.dma_start(
                 tab_s[32 * q : 32 * q + 4 * PASSES, :].bitcast(I32), tab_scales[:, 4 * q : 4 * q + 4, :].bitcast(I32)
@@ -57,40 +57,40 @@ def tile_list_coating_adhesion_chart_kernel(
             )
         w4_w_raw = keep.tile([P, PASSES, H // 2], I32, name="w4_w_raw", align_bytes=64)
         nc.sync.dma_start(w4_w_raw[:], w4_words.bitcast(I32).rearrange("a p w -> p a w"))
-        w1_raw = []
-        for a in range(PASSES):
-            wr = keep.tile([P, PACK, H], F32, name=f"w1_raw{a}")
+
+        def load_w1(a, tag):
+            wr = keep.tile([P, PACK, H], F32, name=f"w1_raw{a}", tag=tag, align_bytes=64)
             nc.sync.dma_start(wr[:], w1[512 * a : 512 * (a + 1), :].rearrange("(p j) c -> p j c", j=PACK))
-            w1_raw.append(wr)
+            return wr
 
         page_rows = page0.rearrange("(q t e) c -> t q e c", t=PACK, e=2)
         wgs_rows = wgs.rearrange("(q t e) j -> t q e j", t=PACK, e=2)
+
+        def load_page(t, tag):
+            pg = keep.tile([P, T2], F32, name=f"page{t}", tag=tag, align_bytes=64)
+            nc.sync.dma_start(pg[:], page_rows[t])
+            return pg
+
+        def load_wgs(t, tag):
+            wg = keep.tile([P, S], F32, name=f"wgs{t}", tag=tag, align_bytes=64)
+            for q in (0, 2, 1, 3):
+                nc.sync.dma_start(wg[32 * q : 32 * (q + 1), :], wgs_rows[t])
+            return wg
+
+        def load_per_row(vec, name, tag):
+            sb = keep.tile([P, PACK], F32, name=name, tag=tag, align_bytes=64)
+            with nc.allow_non_contiguous_dma(reason="one value for each row of the page"):
+                for e in range(2):
+                    nc.sync.dma_start(sb[e:P:2, :], vec.rearrange("(q t e) -> e q t", t=PACK, e=2)[e])
+            return sb
+
+        w1_raw = [load_w1(0, "w1_raw0"), load_w1(1, "w1_raw1")]
         put = keep.tile([P, S // 16], U16, name="put")
         take1 = keep.tile([P, NP // 16], U16, name="take1")
         take2 = keep.tile([P, NP // 16], U16, name="take2")
-        base_sb = keep.tile([P, PACK], F32, name="base_sb")
-        gain_sb = keep.tile([P, PACK], F32, name="gain_sb")
-        pages, weights = [], []
-        for t in range(PACK):
-            wg = keep.tile([P, S], F32, name=f"wgs{t}")
-            for q in range(QUADS):
-                nc.sync.dma_start(wg[32 * q : 32 * (q + 1), :], wgs_rows[t])
-            weights.append(wg)
-            if t == 0:
-                nc.sync.dma_start(put[:], offs2)
-            pg = keep.tile([P, T2], F32, name=f"page{t}")
-            nc.sync.dma_start(pg[:], page_rows[t])
-            pages.append(pg)
-            if t == 0:
-                nc.sync.dma_start(take1[:], offs3)
-                nc.sync.dma_start(take2[:], offs4)
-            if t == 1:
-                with nc.allow_non_contiguous_dma(reason="one value for each row of the page"):
-                    for e in range(2):
-                        nc.sync.dma_start(base_sb[e:P:2, :], base.rearrange("(q t e) -> e q t", t=PACK, e=2)[e])
-                        nc.sync.dma_start(gain_sb[e:P:2, :], gain.rearrange("(q t e) -> e q t", t=PACK, e=2)[e])
-        pair_sb = keep.tile([P, NP // P, NP], F32, name="pair_sb")
-        nc.sync.dma_start(pair_sb[:], pair.rearrange("(c p) j -> p c j", p=P))
+        nc.sync.dma_start(put[:], offs2)
+        nc.sync.dma_start(take1[:], offs3)
+        nc.sync.dma_start(take2[:], offs4)
 
         v_s_low = []
         for a in range(1, PASSES):
@@ -103,51 +103,45 @@ def tile_list_coating_adhesion_chart_kernel(
             nc.vector.tensor_copy(vw[:], tab_w[a][:].bitcast(U32).indirect(pick[:]))
             return vw
 
-        v_w = [gather_words(0, "v_w0")]
-        v_s = keep.tile([P, S], U8, name="v_s", tag="tab_w0", align_bytes=64)
+        v_s = keep.tile([P, S], U8, name="v_s", align_bytes=64)
         nc.vector.tensor_copy(v_s[:], tab_s[:].indirect(pick[:]))
         v_s0 = [v_s] + v_s_low
         for a in range(1, PASSES):
-            nc.gpsimd.dma_start(v_s0[a][0:112, :].bitcast(I32), v_s[4 * a : 4 * a + 112, :].bitcast(I32))
-        v_w.append(gather_words(1, "tab_s"))
+            nc.scalar.dma_start(v_s0[a][0:112, :].bitcast(I32), v_s[4 * a : 4 * a + 112, :].bitcast(I32))
+        v_w = [gather_words(0, "tab_s")]
+        w1_raw.append(load_w1(2, "tab_w0"))
+        v_w.append(gather_words(1, "v_w1"))
+        pages = {0: load_page(0, "tab_w1")}
 
-        w4_w = keep.tile([P, PASSES * 2 * H], U8, name="w4_w", tag="tab_w1", align_bytes=64)
+        w4_s = keep.tile([P, PASSES * H], U8, name="w4_s", align_bytes=64)
         nc.vector.tensor_copy(
-            w4_w[:].bitcast(I32).rearrange("p (a t q) -> p a q t", a=PASSES, t=PACK),
-            w4_w_raw[:].rearrange("p a (q t) -> p a q t", t=PACK),
+            w4_s[:].bitcast(U16).rearrange("p (a t u q) -> p u a q t", a=PASSES, t=PACK, u=2),
+            w4_s_raw[:].bitcast(U16).rearrange("p a (u q t) -> p u a q t", t=PACK, u=2),
         )
-        w4_s = keep.tile([P, PASSES * H], U8, name="w4_s", tag="w4_w_raw", align_bytes=64)
+        weights = {0: load_wgs(0, "w4_s_raw")}
+        w4_w = keep.tile([P, PASSES * 2 * H], U8, name="w4_w", align_bytes=64)
         nc.vector.tensor_copy(
-            w4_s[:].bitcast(U16).rearrange("p (a t q) -> p a q t", a=PASSES, t=PACK),
-            w4_s_raw[:].bitcast(U16).rearrange("p a (q t) -> p a q t", t=PACK),
+            w4_w[:].bitcast(I32).rearrange("p (a t u q) -> p u a q t", a=PASSES, t=PACK, u=2),
+            w4_w_raw[:].rearrange("p a (u q t) -> p u a q t", t=PACK, u=2),
         )
 
-        v_w.append(gather_words(2, "w4_s_raw"))
-
-        w1_bf = {}
-
-        def round_w1(a, t):
-            tag = f"stage{a - 1}" if t == 0 and a > 0 else f"w1_bf{a}_{t}"
+        def quantise_w1(a, t):
+            tag = f"stage{t}" if a == PASSES - 1 and t < 2 else f"w1_bf{a}_{t}"
             rounded = keep.tile([P, P * PACK], BF16, name=f"w1_bf{a}_{t}", tag=tag, align_bytes=64)
             nc.scalar.copy(
                 rounded[:].rearrange("p (q e j) -> p q j e", e=2, j=PACK),
                 w1_raw[a][:].rearrange("p j (q t e) -> p t q j e", t=PACK, e=2)[:, t],
             )
-            w1_bf[a, t] = rounded
+            codes = keep.tile([P, P], U32, name=f"w1_c{a}_{t}", align_bytes=64)
+            plane = keep.tile([P, P], U8, name=f"w1_s{a}_{t}", align_bytes=64)
+            nc.vector.quantize_mx(out=codes[:].bitcast(FP8X4), scales=plane[:], in_=rounded[:])
+            return codes, plane
 
-        def quantise_w1(t):
-            codes = keep.tile([P, PASSES * P], U32, name=f"w1_c{t}", tag="tab_w2", align_bytes=64)
-            planes = keep.tile([P, PASSES * P], U8, name=f"w1_s{t}", tag="w1_s", align_bytes=64)
-            for a in range(PASSES):
-                cols = slice(a * P, (a + 1) * P)
-                nc.vector.quantize_mx(out=codes[:, cols].bitcast(FP8X4), scales=planes[:, cols], in_=w1_bf[a, t][:])
-            return codes, planes
-
-        def first_stage(t, codes, planes):
+        def first_stage(t):
             h2_sb = []
             for half in range(S // BANK):
                 cols = slice(half * BANK, (half + 1) * BANK)
-                h2 = psum.tile([P, BANK], F32, name="h2", tag=f"acc{min(t, 1)}")
+                h2 = psum.tile([P, BANK], F32, name="h2")
                 for a in range(PASSES):
                     g = a * PACK + t
                     nc.tensor.matmul_mx(
@@ -159,18 +153,19 @@ def tile_list_coating_adhesion_chart_kernel(
                         start=(a == 0),
                         stop=(a == PASSES - 1),
                     )
-                hs = keep.tile([P, BANK], F32, name="h2_sb", tag=f"stage{half}", align_bytes=64)
-                nc.scalar.copy(hs[:], h2[:])
-                h2_sb.append(hs)
+                staged = keep.tile([P, BANK], F32, name="h2_sb", tag=f"stage{half}", align_bytes=64)
+                nc.scalar.copy(staged[:], h2[:])
+                h2_sb.append(staged)
             h = keep.tile([P, S], F32, name="h")
             for half in range(S // BANK):
                 cols = slice(half * BANK, (half + 1) * BANK)
-                h1 = psum.tile([P, BANK], F32, name="h1", tag=f"acc{1 - min(t, 1)}")
+                h1 = psum.tile([P, BANK], F32, name="h1")
                 for a in range(PASSES):
+                    codes, plane = w1_mx[a, t]
                     nc.tensor.matmul_mx(
                         out=h1[:],
-                        lhsT=codes[:, a * P : (a + 1) * P].bitcast(FP8X4),
-                        lhsT_scale=planes[:, a * P : (a + 1) * P],
+                        lhsT=codes[:].bitcast(FP8X4),
+                        lhsT_scale=plane[:],
                         rhs=v_w[a][:, cols].bitcast(FP8X4),
                         rhs_scale=v_s[4 * a : P, cols],
                         start=(a == 0),
@@ -182,55 +177,74 @@ def tile_list_coating_adhesion_chart_kernel(
         def put_rows(t, h):
             nc.vector.tensor_tensor(pages[t][:].indirect(put[:]), h[:], weights[t][:], ALU.mult)
 
-        x1 = keep.tile([P, NP, PACK], BF16, name="x1", align_bytes=64)
-        x2 = keep.tile([P, NP, PACK], BF16, name="x2", align_bytes=64)
+        HALF = NP // 2
+        x1 = [keep.tile([P, HALF, PACK], BF16, name=f"x1_{i}", align_bytes=64) for i in range(2)]
+        x2 = [keep.tile([P, HALF, PACK], BF16, name=f"x2_{i}", align_bytes=64) for i in range(2)]
 
         def take_rows(t):
-            pieces = 2 if t == PACK - 1 else 1
-            width = NP // pieces
-            g2 = keep.tile([P, NP], F32, name="g2", tag="stage0", align_bytes=64)
-            g1 = keep.tile([P, NP], F32, name="g1", tag="stage1", align_bytes=64)
-            above = ring.tile([P, NP], F32, name="above")
-            for i in range(pieces):
-                cols = slice(i * width, (i + 1) * width)
-                entries = slice(i * width // 16, (i + 1) * width // 16)
-                nc.vector.tensor_copy(g2[:, cols], pages[t][:].indirect(take2[:, entries]))
-                nc.scalar.activation(above[:, cols], g2[:, cols], ACT.Identity, bias=base_sb[:, t : t + 1], scale=-1.0)
-                nc.scalar.activation(x2[:, cols, t], above[:, cols], ACT.Copy, scale=gain_sb[:, t : t + 1])
-            for i in range(pieces):
-                cols = slice(i * width, (i + 1) * width)
-                entries = slice(i * width // 16, (i + 1) * width // 16)
-                nc.vector.tensor_copy(g1[:, cols], pages[t][:].indirect(take1[:, entries]))
-                nc.scalar.copy(x1[:, cols, t], g1[:, cols])
+            last = t == PACK - 1
+            width = HALF if last else NP
+            got2 = keep.tile([P, NP], F32, name="got2", tag="stage1" if last else "stage0", align_bytes=64)
+            for start in range(0, NP, width):
+                nc.vector.tensor_copy(
+                    got2[:, start : start + width], pages[t][:].indirect(take2[:, start // 16 : (start + width) // 16])
+                )
+            below = ring.tile([P, NP], F32, name="below")
+            for i in range(2):
+                cols = slice(i * HALF, (i + 1) * HALF)
+                nc.scalar.activation(below[:, cols], got2[:, cols], ACT.Identity, bias=base_sb[:, t : t + 1], scale=-1.0)
+                nc.scalar.activation(x2[i][:, :, t], below[:, cols], ACT.Copy, scale=gain_sb[:, t : t + 1])
+            if last:
+                for i in range(2):
+                    nc.vector.tensor_copy(
+                        x1[i][:, :, t], pages[t][:].indirect(take1[:, i * HALF // 16 : (i + 1) * HALF // 16])
+                    )
+            else:
+                got1 = keep.tile([P, NP], F32, name="got1", tag="stage1", align_bytes=64)
+                nc.vector.tensor_copy(got1[:], pages[t][:].indirect(take1[:]))
+                for i in range(2):
+                    nc.scalar.copy(x1[i][:, :, t], got1[:, i * HALF : (i + 1) * HALF])
 
-        for a in range(PASSES - 1):
-            round_w1(a, 0)
-            round_w1(a, 1)
-        round_w1(PASSES - 1, 0)
-        h_now = first_stage(0, *quantise_w1(0))
-        round_w1(PASSES - 1, 1)
-        w1_next = quantise_w1(1)
+        w1_mx = {(0, 0): quantise_w1(0, 0)}
+        v_w.append(gather_words(2, "w1_bf0_0"))
+        for a in range(1, PASSES):
+            w1_mx[a, 0] = quantise_w1(a, 0)
+        for a in range(PASSES):
+            w1_mx[a, 1] = quantise_w1(a, 1)
+        h_now = first_stage(0)
+        for t in range(2, PACK):
+            for a in range(PASSES):
+                w1_mx[a, t] = quantise_w1(a, t)
+        base_sb = load_per_row(base, "base_sb", "w1_bf1_3")
+        gain_sb = load_per_row(gain, "gain_sb", "w1_bf2_3")
+        pages[1] = load_page(1, "w1_raw1")
+        weights[1] = load_wgs(1, "tab_w0")
+        pages[2] = load_page(2, "w1_bf2_2")
         put_rows(0, h_now)
-        for t in range(PACK):
-            h_next = first_stage(t + 1, *w1_next) if t + 1 < PACK else None
-            if t + 2 < PACK:
-                for a in range(PASSES):
-                    round_w1(a, t + 2)
-                w1_next = quantise_w1(t + 2)
-            take_rows(t)
-            if h_next is not None:
-                put_rows(t + 1, h_next)
+        weights[2] = load_wgs(2, "w4_s_raw")
+        for t in range(1, PACK):
+            h_now = first_stage(t)
+            take_rows(t - 1)
+            if t == 1:
+                pages[3] = load_page(3, "tab_w1")
+            if t == 2:
+                pair_sb = keep.tile([P, NP // P, NP], F32, name="pair_sb", tag="w1_raw1", align_bytes=64)
+                nc.sync.dma_start(pair_sb[:], pair.rearrange("(c p) j -> p c j", p=P))
+            put_rows(t, h_now)
+            if t == 1:
+                weights[3] = load_wgs(3, "tab_w0")
+        take_rows(PACK - 1)
 
         x2_c = keep.tile([P, NP], U32, name="x2_c", align_bytes=64)
         x2_s = keep.tile([P, NP], U8, name="x2_s", align_bytes=64)
-        nc.vector.quantize_mx(out=x2_c[:].bitcast(FP8X4), scales=x2_s[:], in_=x2[:].rearrange("p m t -> p (m t)"))
         x1_c = keep.tile([P, NP], U32, name="x1_c", align_bytes=64)
         x1_s = keep.tile([P, NP], U8, name="x1_s", align_bytes=64)
-        for c in range(NP // P):
-            rows = slice(c * P, (c + 1) * P)
-            nc.vector.quantize_mx(
-                out=x1_c[:, rows].bitcast(FP8X4), scales=x1_s[:, rows], in_=x1[:, rows, :].rearrange("p m t -> p (m t)")
-            )
+        for halves, codes, plane in ((x2, x2_c, x2_s), (x1, x1_c, x1_s)):
+            for i in range(2):
+                cols = slice(i * HALF, (i + 1) * HALF)
+                nc.vector.quantize_mx(
+                    out=codes[:, cols].bitcast(FP8X4), scales=plane[:, cols], in_=halves[i][:].rearrange("p m t -> p (m t)")
+                )
         for c in range(NP // P):
             rows = slice(c * P, (c + 1) * P)
             e = psum.tile([P, NP], F32, name="e", bufs=4)
@@ -244,7 +258,10 @@ def tile_list_coating_adhesion_chart_kernel(
                 stop=True,
             )
             bounded = ring.tile([P, NP], F32, name="bounded", bufs=4)
-            nc.scalar.activation(bounded[:], e[:], ACT.Tanh, scale=-1.0)
             chart = ring.tile([P, NP], F32, name="chart", bufs=4)
-            nc.vector.tensor_tensor(chart[:], bounded[:], pair_sb[:, c, :], ALU.mult)
-            nc.sync.dma_start(out[rows, :], chart[:])
+            width = HALF if c == NP // P - 1 else NP
+            for start in range(0, NP, width):
+                cols = slice(start, start + width)
+                nc.scalar.activation(bounded[:, cols], e[:, cols], ACT.Tanh, scale=-1.0)
+                nc.vector.tensor_tensor(chart[:, cols], bounded[:, cols], pair_sb[:, c, cols], ALU.mult)
+                nc.sync.dma_start(out[rows, cols], chart[:, cols])

from contextlib import ExitStack

import concourse.mybir as mybir

K, T, S, H, T2, NP = 1536, 2048, 1024, 512, 2048, 512
FLOPS = 2 * (2 * K * H * S + H * NP * NP)

F32 = mybir.dt.float32
BF16 = mybir.dt.bfloat16
I32 = mybir.dt.int32
U32 = mybir.dt.uint32
U16 = mybir.dt.uint16
U8 = mybir.dt.uint8
FP8X4 = mybir.dt.float8_e4m3fn_x4
FP4X4 = mybir.dt.float4_e2m1fn_x4
ALU = mybir.AluOpType
ACT = mybir.ActivationFunctionType

P = 128
PACK = 4
PASSES = K // (P * PACK)
BANK = 512
QUADS = 4


def tile_list_coating_adhesion_chart_kernel(
    tc, tab_words, tab_scales, offs, w1, w4_words, w4_scales, page0, offs2, wgs, offs3, offs4, base, gain, pair, out
):
    nc = tc.nc
    with ExitStack() as ctx:
        keep = ctx.enter_context(tc.tile_pool(name="keep", bufs=1))
        ring = ctx.enter_context(tc.tile_pool(name="ring", bufs=2))
        psum = ctx.enter_context(tc.psum_pool(name="psum", bufs=2))

        pick = keep.tile([P, S // 16], U16, name="pick")
        nc.sync.dma_start(pick[:], offs)

        def load_table(a):
            tw = keep.tile([P, T], I32, name=f"tab_w{a}", align_bytes=64)
            nc.sync.dma_start(tw[:], tab_words[a].rearrange("p t i -> p (t i)").bitcast(I32))
            return tw

        tab_w = [load_table(0)]
        tab_s = keep.tile([P, T], U8, name="tab_s", align_bytes=64)
        nc.gpsimd.memset(tab_s[:].bitcast(I32), 0)
        w4_s_raw = keep.tile([P, PASSES, H], U8, name="w4_s_raw", align_bytes=64)
        nc.gpsimd.memset(w4_s_raw[:].bitcast(I32), 0)
        for q in range(QUADS):
            nc.sync.dma_start(
                tab_s[32 * q : 32 * q + 4 * PASSES, :].bitcast(I32), tab_scales[:, 4 * q : 4 * q + 4, :].bitcast(I32)
            )
        tab_w.extend(load_table(a) for a in range(1, PASSES))
        for q in range(QUADS):
            nc.sync.dma_start(
                w4_s_raw[32 * q : 32 * q + 4, :, :].bitcast(I32),
                w4_scales[:, 4 * q : 4 * q + 4, :].rearrange("a r c -> r a c").bitcast(I32),
            )
        w4_w_raw = keep.tile([P, PASSES, H // 2], I32, name="w4_w_raw", align_bytes=64)
        nc.sync.dma_start(w4_w_raw[:], w4_words.bitcast(I32).rearrange("a p w -> p a w"))

        def load_w1(a, tag):
            wr = keep.tile([P, PACK, H], F32, name=f"w1_raw{a}", tag=tag, align_bytes=64)
            nc.sync.dma_start(wr[:], w1[512 * a : 512 * (a + 1), :].rearrange("(p j) c -> p j c", j=PACK))
            return wr

        page_rows = page0.rearrange("(q t e) c -> t q e c", t=PACK, e=2)
        wgs_rows = wgs.rearrange("(q t e) j -> t q e j", t=PACK, e=2)

        def load_page(t, tag):
            pg = keep.tile([P, T2], F32, name=f"page{t}", tag=tag, align_bytes=64)
            nc.sync.dma_start(pg[:], page_rows[t])
            return pg

        def load_wgs(t, tag):
            wg = keep.tile([P, S], F32, name=f"wgs{t}", tag=tag, align_bytes=64)
            for q in (0, 2, 1, 3):
                nc.sync.dma_start(wg[32 * q : 32 * (q + 1), :], wgs_rows[t])
            return wg

        def load_per_row(vec, name, tag):
            sb = keep.tile([P, PACK], F32, name=name, tag=tag, align_bytes=64)
            with nc.allow_non_contiguous_dma(reason="one value for each row of the page"):
                for e in range(2):
                    nc.sync.dma_start(sb[e:P:2, :], vec.rearrange("(q t e) -> e q t", t=PACK, e=2)[e])
            return sb

        w1_raw = [load_w1(0, "w1_raw0"), load_w1(1, "w1_raw1")]
        put = keep.tile([P, S // 16], U16, name="put")
        take1 = keep.tile([P, NP // 16], U16, name="take1")
        take2 = keep.tile([P, NP // 16], U16, name="take2")
        nc.sync.dma_start(put[:], offs2)
        nc.sync.dma_start(take1[:], offs3)
        nc.sync.dma_start(take2[:], offs4)

        v_s_low = []
        for a in range(1, PASSES):
            sh = keep.tile([P, S], U8, name=f"v_s_low{a}", align_bytes=64)
            nc.vector.memset(sh[:].bitcast(I32), 0)
            v_s_low.append(sh)

        def gather_words(a, tag):
            vw = keep.tile([P, S], U32, name=f"v_w{a}", tag=tag, align_bytes=64)
            nc.vector.tensor_copy(vw[:], tab_w[a][:].bitcast(U32).indirect(pick[:]))
            return vw

        v_s = keep.tile([P, S], U8, name="v_s", align_bytes=64)
        nc.vector.tensor_copy(v_s[:], tab_s[:].indirect(pick[:]))
        v_s0 = [v_s] + v_s_low
        for a in range(1, PASSES):
            nc.scalar.dma_start(v_s0[a][0:112, :].bitcast(I32), v_s[4 * a : 4 * a + 112, :].bitcast(I32))
        v_w = [gather_words(0, "tab_s")]
        w1_raw.append(load_w1(2, "tab_w0"))
        v_w.append(gather_words(1, "v_w1"))
        pages = {0: load_page(0, "tab_w1")}

        w4_s = keep.tile([P, PASSES * H], U8, name="w4_s", align_bytes=64)
        nc.vector.tensor_copy(
            w4_s[:].bitcast(U16).rearrange("p (a t u q) -> p u a q t", a=PASSES, t=PACK, u=2),
            w4_s_raw[:].bitcast(U16).rearrange("p a (u q t) -> p u a q t", t=PACK, u=2),
        )
        weights = {0: load_wgs(0, "w4_s_raw")}
        w4_w = keep.tile([P, PASSES * 2 * H], U8, name="w4_w", align_bytes=64)
        nc.vector.tensor_copy(
            w4_w[:].bitcast(I32).rearrange("p (a t u q) -> p u a q t", a=PASSES, t=PACK, u=2),
            w4_w_raw[:].rearrange("p a (u q t) -> p u a q t", t=PACK, u=2),
        )

        def quantise_w1(a, t):
            tag = f"stage{t}" if a == PASSES - 1 and t < 2 else f"w1_bf{a}_{t}"
            rounded = keep.tile([P, P * PACK], BF16, name=f"w1_bf{a}_{t}", tag=tag, align_bytes=64)
            nc.scalar.copy(
                rounded[:].rearrange("p (q e j) -> p q j e", e=2, j=PACK),
                w1_raw[a][:].rearrange("p j (q t e) -> p t q j e", t=PACK, e=2)[:, t],
            )
            codes = keep.tile([P, P], U32, name=f"w1_c{a}_{t}", align_bytes=64)
            plane = keep.tile([P, P], U8, name=f"w1_s{a}_{t}", align_bytes=64)
            nc.vector.quantize_mx(out=codes[:].bitcast(FP8X4), scales=plane[:], in_=rounded[:])
            return codes, plane

        def first_stage(t):
            h2_sb = []
            for half in range(S // BANK):
                cols = slice(half * BANK, (half + 1) * BANK)
                h2 = psum.tile([P, BANK], F32, name="h2")
                for a in range(PASSES):
                    g = a * PACK + t
                    nc.tensor.matmul_mx(
                        out=h2[:],
                        lhsT=w4_w[:, 2 * P * g : 2 * P * (g + 1)].bitcast(FP4X4),
                        lhsT_scale=w4_s[:, P * g : P * (g + 1)],
                        rhs=v_w[a][:, cols].bitcast(FP8X4),
                        rhs_scale=v_s0[a][:, cols],
                        start=(a == 0),
                        stop=(a == PASSES - 1),
                    )
                staged = keep.tile([P, BANK], F32, name="h2_sb", tag=f"stage{half}", align_bytes=64)
                nc.scalar.copy(staged[:], h2[:])
                h2_sb.append(staged)
            h = keep.tile([P, S], F32, name="h")
            for half in range(S // BANK):
                cols = slice(half * BANK, (half + 1) * BANK)
                h1 = psum.tile([P, BANK], F32, name="h1")
                for a in range(PASSES):
                    codes, plane = w1_mx[a, t]
                    nc.tensor.matmul_mx(
                        out=h1[:],
                        lhsT=codes[:].bitcast(FP8X4),
                        lhsT_scale=plane[:],
                        rhs=v_w[a][:, cols].bitcast(FP8X4),
                        rhs_scale=v_s[4 * a : P, cols],
                        start=(a == 0),
                        stop=(a == PASSES - 1),
                    )
                nc.vector.tensor_tensor(h[:, cols], h1[:], h2_sb[half][:], ALU.max)
            return h

        def put_rows(t, h):
            nc.vector.tensor_tensor(pages[t][:].indirect(put[:]), h[:], weights[t][:], ALU.mult)

        HALF = NP // 2
        x1 = [keep.tile([P, HALF, PACK], BF16, name=f"x1_{i}", align_bytes=64) for i in range(2)]
        x2 = [keep.tile([P, HALF, PACK], BF16, name=f"x2_{i}", align_bytes=64) for i in range(2)]

        def take_rows(t):
            last = t == PACK - 1
            width = HALF if last else NP
            got2 = keep.tile([P, NP], F32, name="got2", tag="stage1" if last else "stage0", align_bytes=64)
            for start in range(0, NP, width):
                nc.vector.tensor_copy(
                    got2[:, start : start + width], pages[t][:].indirect(take2[:, start // 16 : (start + width) // 16])
                )
            below = ring.tile([P, NP], F32, name="below")
            for i in range(2):
                cols = slice(i * HALF, (i + 1) * HALF)
                nc.scalar.activation(below[:, cols], got2[:, cols], ACT.Identity, bias=base_sb[:, t : t + 1], scale=-1.0)
                nc.scalar.activation(x2[i][:, :, t], below[:, cols], ACT.Copy, scale=gain_sb[:, t : t + 1])
            if last:
                for i in range(2):
                    nc.vector.tensor_copy(
                        x1[i][:, :, t], pages[t][:].indirect(take1[:, i * HALF // 16 : (i + 1) * HALF // 16])
                    )
            else:
                got1 = keep.tile([P, NP], F32, name="got1", tag="stage1", align_bytes=64)
                nc.vector.tensor_copy(got1[:], pages[t][:].indirect(take1[:]))
                for i in range(2):
                    nc.scalar.copy(x1[i][:, :, t], got1[:, i * HALF : (i + 1) * HALF])

        w1_mx = {(0, 0): quantise_w1(0, 0)}
        v_w.append(gather_words(2, "w1_bf0_0"))
        for a in range(1, PASSES):
            w1_mx[a, 0] = quantise_w1(a, 0)
        for a in range(PASSES):
            w1_mx[a, 1] = quantise_w1(a, 1)
        h_now = first_stage(0)
        for t in range(2, PACK):
            for a in range(PASSES):
                w1_mx[a, t] = quantise_w1(a, t)
        base_sb = load_per_row(base, "base_sb", "w1_bf1_3")
        gain_sb = load_per_row(gain, "gain_sb", "w1_bf2_3")
        pages[1] = load_page(1, "w1_raw1")
        weights[1] = load_wgs(1, "tab_w0")
        pages[2] = load_page(2, "w1_bf2_2")
        put_rows(0, h_now)
        weights[2] = load_wgs(2, "w4_s_raw")
        for t in range(1, PACK):
            h_now = first_stage(t)
            take_rows(t - 1)
            if t == 1:
                pages[3] = load_page(3, "tab_w1")
            if t == 2:
                pair_sb = keep.tile([P, NP // P, NP], F32, name="pair_sb", tag="w1_raw1", align_bytes=64)
                nc.sync.dma_start(pair_sb[:], pair.rearrange("(c p) j -> p c j", p=P))
            put_rows(t, h_now)
            if t == 1:
                weights[3] = load_wgs(3, "tab_w0")
        take_rows(PACK - 1)

        x2_c = keep.tile([P, NP], U32, name="x2_c", align_bytes=64)
        x2_s = keep.tile([P, NP], U8, name="x2_s", align_bytes=64)
        x1_c = keep.tile([P, NP], U32, name="x1_c", align_bytes=64)
        x1_s = keep.tile([P, NP], U8, name="x1_s", align_bytes=64)
        for halves, codes, plane in ((x2, x2_c, x2_s), (x1, x1_c, x1_s)):
            for i in range(2):
                cols = slice(i * HALF, (i + 1) * HALF)
                nc.vector.quantize_mx(
                    out=codes[:, cols].bitcast(FP8X4), scales=plane[:, cols], in_=halves[i][:].rearrange("p m t -> p (m t)")
                )
        for c in range(NP // P):
            rows = slice(c * P, (c + 1) * P)
            e = psum.tile([P, NP], F32, name="e", bufs=4)
            nc.tensor.matmul_mx(
                out=e[:],
                lhsT=x1_c[:, rows].bitcast(FP8X4),
                lhsT_scale=x1_s[:, rows],
                rhs=x2_c[:].bitcast(FP8X4),
                rhs_scale=x2_s[:],
                start=True,
                stop=True,
            )
            bounded = ring.tile([P, NP], F32, name="bounded", bufs=4)
            chart = ring.tile([P, NP], F32, name="chart", bufs=4)
            width = HALF if c == NP // P - 1 else NP
            for start in range(0, NP, width):
                cols = slice(start, start + width)
                nc.scalar.activation(bounded[:, cols], e[:, cols], ACT.Tanh, scale=-1.0)
                nc.vector.tensor_tensor(chart[:, cols], bounded[:, cols], pair_sb[:, c, cols], ALU.mult)
                nc.sync.dma_start(out[rows, cols], chart[:, cols])
